import numpy as np
import ml_dtypes


def mxq(x, axis, fmt="e4m3"):
    dtype, down = {"e4m3": (ml_dtypes.float8_e4m3fn, 7), "e5m2": (ml_dtypes.float8_e5m2, 14)}[fmt]
    v = np.moveaxis(np.asarray(x, np.float32).astype(ml_dtypes.bfloat16).astype(np.float64), axis, -1)
    blocks = v.reshape(v.shape[:-1] + (-1, 32))
    amax = np.abs(blocks).max(-1, keepdims=True)
    byte = np.maximum(np.where(amax > 0, np.frexp(amax)[1] - 1 + 127, 0) - down, 1)
    scale = np.exp2(byte - 127.0)
    codes = (blocks / scale).astype(np.float32).astype(dtype).astype(np.float64)
    return np.moveaxis((codes * scale).reshape(v.shape), -1, axis)


WIDE = False


def mx_kscale(k):
    if not WIDE:
        return np.ones(k)
    levels = np.array([10, -10, 5, -5, 0])
    if k % 512:
        return np.exp2(np.random.permutation(np.resize(levels, k // 32))).repeat(32)
    a = np.empty((k // 512, 16))
    for p in range(k // 512):
        a[p, :8] = np.random.permutation(np.resize(levels, 8))
        for g in range(8):
            far = levels[np.abs(levels - a[p, g]) >= 10]
            a[p, g + 8] = far[np.random.randint(len(far))]
    return np.exp2(a.ravel()).repeat(32)


def f64(x):
    return np.asarray(x).astype(np.float64)


def striped(idx):
    return np.tile(idx.reshape(-1, 16).T, (8, 1)).astype(np.uint16)


def unstriped(offs):
    return offs[:16].T.reshape(-1).astype(np.int64)


def sigmoid(v):
    return 1.0 / (1.0 + np.exp(-np.maximum(v, -700.0)))

def planes(y):
    n, m = y.shape
    v = y.astype(np.float32).astype(ml_dtypes.bfloat16).astype(np.float64).reshape(n // 32, 32, m)
    top = np.abs(v).max(1)
    byte = np.clip(np.where(top > 0, np.frexp(top)[1] - 1 + 127 - 7, 1), 1, 254)
    codes = (v * np.exp2(127.0 - byte)[:, None, :]).reshape(n, m).astype(np.float32).astype(ml_dtypes.float8_e4m3fn).view(np.uint8)
    words = codes.reshape(n // 512, 128, 4, m).transpose(0, 1, 3, 2)
    return np.ascontiguousarray(words), np.ascontiguousarray(byte.astype(np.uint8).reshape(n // 512, 16, m))


K, T, S, V, N = 512, 1024, 512, 256, 512


def setup_inputs():
    n = np.random.standard_normal
    s = mx_kscale(K)[:, None]
    return {
        "xT": (n((K, T)) * s).astype(np.float32),
        "w1": (n((K, N)) / np.sqrt(K) / s).astype(np.float32),
        "offs": striped(np.random.permutation(T)[:S]),
        "win": striped(np.random.permutation(S)[:V]),
        "lose": striped(np.random.permutation(S)[:V]),
    }


def reference(xT, w1, offs, win, lose):
    xq = mxq(f64(xT)[:, unstriped(offs)], 0, "e4m3")
    y = mxq(f64(w1), 0, "e4m3").T @ xq
    out_0 = sigmoid(y[:, unstriped(win)] - y[:, unstriped(lose)])
    return (out_0,) + planes(out_0)

@@ -1,0 +1,137 @@
+from contextlib import ExitStack
+
+import concourse.mybir as mybir
+
+K, T, S, V, N = 512, 1024, 512, 256, 512
+FLOPS = 2 * K * N * S
+
+F32 = mybir.dt.float32
+BF16 = mybir.dt.bfloat16
+I32 = mybir.dt.int32
+U32 = mybir.dt.uint32
+U16 = mybir.dt.uint16
+U8 = mybir.dt.uint8
+FP8X4 = mybir.dt.float8_e4m3fn_x4
+ACT = mybir.ActivationFunctionType
+SUB = mybir.AluOpType.subtract
+
+P = 128
+PACK = 4
+M_TILE = 128
+HALF_S = S // 2
+HALF_V = V // 2
+LIST_ROWS = 16
+
+
+def tile_picked_ranknet_sigmoid_lo_kernel(tc, xT, w1, offs, win, lose, out_0, out_1, out_2):
+    nc = tc.nc
+    with ExitStack() as ctx:
+        lists = ctx.enter_context(tc.tile_pool(name="lists", bufs=1))
+        keep = ctx.enter_context(tc.tile_pool(name="keep", bufs=1))
+        psum = ctx.enter_context(tc.psum_pool(name="psum", bufs=1))
+
+        offs_sb = lists.tile([P, S // LIST_ROWS], U16, name="offs_sb")
+        win_sb = lists.tile([P, V // LIST_ROWS], U16, name="win_sb")
+        lose_sb = lists.tile([P, V // LIST_ROWS], U16, name="lose_sb")
+
+        x_rows = xT.rearrange("(p j) t -> p j t", j=PACK)
+        x_f32 = [keep.tile([P, T], F32, name="x_f32_%d" % j) for j in range(PACK)]
+        w_f32 = keep.tile([P, PACK, N], F32, name="w_f32")
+        load_order = (0, 2, 1, 3)
+        nc.sync.dma_start(x_f32[0][:], x_rows[:, 0, :])
+        nc.sync.dma_start(offs_sb[:], offs)
+        for j in load_order[1:]:
+            nc.sync.dma_start(x_f32[j][:], x_rows[:, j, :])
+        nc.sync.dma_start(w_f32[:], w1.rearrange("(p j) n -> p j n", j=PACK))
+        nc.sync.dma_start(lose_sb[:], lose)
+        nc.sync.dma_start(win_sb[:], win)
+
+        warm_in = keep.tile([P, 1], F32, name="warm_in")
+        warm_out = keep.tile([P, 1], F32, name="warm_out")
+        nc.vector.memset(warm_in[:], 0.0)
+        nc.scalar.activation(warm_out[:], warm_in[:], ACT.Sigmoid)
+
+        x_grouped = keep.tile([P, S, PACK], BF16, name="x_grouped", align_bytes=64)
+        for j in load_order:
+            if j < 2:
+                x_bf16 = keep.tile([P, T], BF16, name="x_bf16_%d" % j)
+                nc.vector.tensor_copy(x_bf16[:], x_f32[j][:])
+                nc.scalar.activation(x_grouped[:, :, j], x_bf16[:].indirect(offs_sb[:]), ACT.Copy)
+            else:
+                nc.vector.tensor_copy(x_grouped[:, :, j], x_f32[j][:].indirect(offs_sb[:]))
+        x_codes = keep.tile([P, S], U32, name="x_codes", align_bytes=64)
+        x_scales = keep.tile([P, S], U8, name="x_scales", align_bytes=64)
+        nc.vector.quantize_mx(out=x_codes[:].bitcast(FP8X4), scales=x_scales[:], in_=x_grouped[:].rearrange("p s j -> p (s j)"))
+
+        w_dealt = w_f32[:].rearrange("p j (m t) -> p m j t", t=PACK)
+        w_codes, w_scales = [], []
+        w_grouped = []
+        for pair, copy in enumerate((nc.vector.tensor_copy, nc.scalar.copy)):
+            g = keep.tile([P, 2, M_TILE, PACK], BF16, name="w_grouped_%d" % pair, align_bytes=64)
+            copy(g[:].rearrange("p t m j -> p m j t"), w_dealt[:, :, :, 2 * pair : 2 * pair + 2])
+            w_grouped.append(g)
+        for pair in range(2):
+            codes = keep.tile([P, 2 * M_TILE], U32, name="w_codes_%d" % pair, align_bytes=64)
+            scales = keep.tile([P, 2 * M_TILE], U8, name="w_scales_%d" % pair, align_bytes=64)
+            nc.vector.quantize_mx(out=codes[:].bitcast(FP8X4), scales=scales[:], in_=w_grouped[pair][:].rearrange("p t m j -> p (t m j)"))
+            w_codes.append(codes)
+            w_scales.append(scales)
+
+        def product(acc, t, cols):
+            m_cols = slice((t % 2) * M_TILE, (t % 2 + 1) * M_TILE)
+            nc.tensor.matmul_mx(
+                out=acc,
+                lhsT=w_codes[t // 2][:, m_cols].bitcast(FP8X4),
+                lhsT_scale=w_scales[t // 2][:, m_cols],
+                rhs=x_codes[:, cols].bitcast(FP8X4),
+                rhs_scale=x_scales[:, cols],
+                start=True,
+                stop=True,
+            )
+
+        y = [keep.tile([P, S], F32, name="y_%d" % t) for t in range(PACK)]
+        for h, copy in enumerate((nc.scalar.copy, nc.vector.tensor_copy)):
+            cols = slice(h * HALF_S, (h + 1) * HALF_S)
+            acc = psum.tile([P, HALF_S], F32, name="acc_0_%d" % h)
+            product(acc[:], 0, cols)
+            copy(y[0][:, cols], acc[:])
+        for t in range(1, PACK):
+            acc = psum.tile([P, S], F32, name="acc_%d" % t)
+            product(acc[:], t, slice(0, S))
+            nc.scalar.copy(y[t][:], acc[:])
+
+        losers = [keep.tile([P, V], F32, name="losers_%d" % t) for t in range(PACK)]
+        margins = [keep.tile([P, V], F32, name="margins_%d" % t) for t in range(PACK)]
+        prob = keep.tile([P, PACK, V], F32, name="prob")
+        out_rows = out_0.rearrange("(p t) v -> p t v", t=PACK)
+
+        def fetch_losers(t):
+            nc.vector.tensor_copy(losers[t][:], y[t][:].indirect(lose_sb[:]))
+
+        def compare(t, v0, v1):
+            offsets = win_sb[:, v0 // LIST_ROWS : v1 // LIST_ROWS]
+            nc.vector.tensor_tensor(margins[t][:, v0:v1], y[t][:].indirect(offsets), losers[t][:, v0:v1], SUB)
+            nc.scalar.activation(prob[:, t, v0:v1], margins[t][:, v0:v1], ACT.Sigmoid)
+
+        fetch_losers(0)
+        for t in range(PACK - 1):
+            fetch_losers(t + 1)
+            compare(t, 0, V)
+            nc.sync.dma_start(out_rows[:, t, :], prob[:, t, :])
+        last = PACK - 1
+        for h in range(2):
+            compare(last, h * HALF_V, (h + 1) * HALF_V)
+        nc.sync.dma_start(out_rows[:, last, :], prob[:, last, :])
+
+        out_codes = keep.tile([P, V], U32, name="out_codes", align_bytes=64)
+        out_scales = keep.tile([P, V], U8, name="out_scales", align_bytes=64)
+        words = out_1[0].rearrange("p v r -> p (v r)").bitcast(I32)
+        halves = [slice(h * HALF_V, (h + 1) * HALF_V) for h in range(2)]
+        grouped = [keep.tile([P, HALF_V, PACK], BF16, name="prob_grouped_%d" % h, align_bytes=64) for h in range(2)]
+        for h, cols in enumerate(halves):
+            nc.vector.tensor_copy(grouped[h][:].rearrange("p (c i) t -> p c t i", i=4), prob[:, :, cols].rearrange("p t (c i) -> p c t i", i=4))
+        for h, cols in enumerate(halves):
+            nc.vector.quantize_mx(out=out_codes[:, cols].bitcast(FP8X4), scales=out_scales[:, cols], in_=grouped[h][:].rearrange("p v t -> p (v t)"))
+            nc.sync.dma_start(words[:, cols], out_codes[:, cols].bitcast(I32))
+        for q, queue in enumerate((nc.scalar, nc.scalar, nc.sync, nc.sync)):
+            queue.dma_start(out_2[0, 4 * q : 4 * q + 4, :].bitcast(I32), out_scales[32 * q : 32 * q + 4, :].bitcast(I32))

@@ -64,25 +64,31 @@ def tile_picked_ranknet_sigmoid_lo_kernel(tc, xT, w1, offs, win, lose, out_0, ou
         nc.vector.quantize_mx(out=x_codes[:].bitcast(FP8X4), scales=x_scales[:], in_=x_grouped[:].rearrange("p s j -> p (s j)"))
 
         w_dealt = w_f32[:].rearrange("p j (m t) -> p m j t", t=PACK)
-        w_codes, w_scales = [], []
-        w_grouped = []
-        for pair, copy in enumerate((nc.vector.tensor_copy, nc.scalar.copy)):
-            g = keep.tile([P, 2, M_TILE, PACK], BF16, name="w_grouped_%d" % pair, align_bytes=64)
-            copy(g[:].rearrange("p t m j -> p m j t"), w_dealt[:, :, :, 2 * pair : 2 * pair + 2])
-            w_grouped.append(g)
-        for pair in range(2):
-            codes = keep.tile([P, 2 * M_TILE], U32, name="w_codes_%d" % pair, align_bytes=64)
-            scales = keep.tile([P, 2 * M_TILE], U8, name="w_scales_%d" % pair, align_bytes=64)
-            nc.vector.quantize_mx(out=codes[:].bitcast(FP8X4), scales=scales[:], in_=w_grouped[pair][:].rearrange("p t m j -> p (t m j)"))
-            w_codes.append(codes)
-            w_scales.append(scales)
+        w_grouped = [keep.tile([P, 2, M_TILE, PACK], BF16, name="w_grouped_%d" % pair, align_bytes=64) for pair in range(2)]
+        w_codes = [keep.tile([P, M_TILE], U32, name="w_codes_%d" % t, align_bytes=64) for t in range(2)]
+        w_scales = [keep.tile([P, M_TILE], U8, name="w_scales_%d" % t, align_bytes=64) for t in range(2)]
+        late_codes = keep.tile([P, 2 * M_TILE], U32, name="late_codes", align_bytes=64)
+        late_scales = keep.tile([P, 2 * M_TILE], U8, name="late_scales", align_bytes=64)
+
+        def deal(pair, split):
+            dst = w_grouped[pair][:].rearrange("p t m j -> p m j t")
+            src = w_dealt[:, :, :, 2 * pair : 2 * pair + 2]
+            nc.vector.tensor_copy(dst[:, :split], src[:, :split])
+            nc.scalar.copy(dst[:, split:], src[:, split:])
+
+        deal(0, 80)
+        for t in range(2):
+            nc.vector.quantize_mx(out=w_codes[t][:].bitcast(FP8X4), scales=w_scales[t][:], in_=w_grouped[0][:, t].rearrange("p m j -> p (m j)"))
+        deal(1, 48)
+        nc.vector.quantize_mx(out=late_codes[:].bitcast(FP8X4), scales=late_scales[:], in_=w_grouped[1][:].rearrange("p t m j -> p (t m j)"))
+        stationary = [(w_codes[t][:], w_scales[t][:]) for t in range(2)]
+        stationary = stationary + [(late_codes[:, u * M_TILE : (u + 1) * M_TILE], late_scales[:, u * M_TILE : (u + 1) * M_TILE]) for u in range(2)]
 
         def product(acc, t, cols):
-            m_cols = slice((t % 2) * M_TILE, (t % 2 + 1) * M_TILE)
             nc.tensor.matmul_mx(
                 out=acc,
-                lhsT=w_codes[t // 2][:, m_cols].bitcast(FP8X4),
-                lhsT_scale=w_scales[t // 2][:, m_cols],
+                lhsT=stationary[t][0].bitcast(FP8X4),
+                lhsT_scale=stationary[t][1],
                 rhs=x_codes[:, cols].bitcast(FP8X4),
                 rhs_scale=x_scales[:, cols],
                 start=True,
@@ -105,28 +111,20 @@ def tile_picked_ranknet_sigmoid_lo_kernel(tc, xT, w1, offs, win, lose, out_0, ou
         prob = keep.tile([P, PACK, V], F32, name="prob")
         out_rows = out_0.rearrange("(p t) v -> p t v", t=PACK)
 
-        def fetch_losers(t):
-            nc.vector.tensor_copy(losers[t][:], y[t][:].indirect(lose_sb[:]))
-
-        def compare(t, v0, v1):
-            offsets = win_sb[:, v0 // LIST_ROWS : v1 // LIST_ROWS]
-            nc.vector.tensor_tensor(margins[t][:, v0:v1], y[t][:].indirect(offsets), losers[t][:, v0:v1], SUB)
-            nc.scalar.activation(prob[:, t, v0:v1], margins[t][:, v0:v1], ACT.Sigmoid)
-
-        fetch_losers(0)
-        for t in range(PACK - 1):
-            fetch_losers(t + 1)
-            compare(t, 0, V)
+        halves = [slice(h * HALF_V, (h + 1) * HALF_V) for h in range(2)]
+        list_halves = [slice(c.start // LIST_ROWS, c.stop // LIST_ROWS) for c in halves]
+        for t in range(PACK):
+            for cols, entries in zip(halves, list_halves):
+                nc.vector.tensor_copy(losers[t][:, cols], y[t][:].indirect(lose_sb[:, entries]))
+            for cols, entries in zip(halves, list_halves):
+                nc.vector.tensor_tensor(margins[t][:, cols], y[t][:].indirect(win_sb[:, entries]), losers[t][:, cols], SUB)
+            for cols in halves if t == PACK - 1 else [slice(0, V)]:
+                nc.scalar.activation(prob[:, t, cols], margins[t][:, cols], ACT.Sigmoid)
             nc.sync.dma_start(out_rows[:, t, :], prob[:, t, :])
-        last = PACK - 1
-        for h in range(2):
-            compare(last, h * HALF_V, (h + 1) * HALF_V)
-        nc.sync.dma_start(out_rows[:, last, :], prob[:, last, :])
 
         out_codes = keep.tile([P, V], U32, name="out_codes", align_bytes=64)
         out_scales = keep.tile([P, V], U8, name="out_scales", align_bytes=64)
         words = out_1[0].rearrange("p v r -> p (v r)").bitcast(I32)
-        halves = [slice(h * HALF_V, (h + 1) * HALF_V) for h in range(2)]
         grouped = [keep.tile([P, HALF_V, PACK], BF16, name="prob_grouped_%d" % h, align_bytes=64) for h in range(2)]
         for h, cols in enumerate(halves):
             nc.vector.tensor_copy(grouped[h][:].rearrange("p (c i) t -> p c t i", i=4), prob[:, :, cols].rearrange("p t (c i) -> p c t i", i=4))

@@ -52,11 +52,17 @@ def tile_picked_ranknet_sigmoid_lo_kernel(tc, xT, w1, offs, win, lose, out_0, ou
         nc.scalar.activation(warm_out[:], warm_in[:], ACT.Sigmoid)
 
         x_grouped = keep.tile([P, S, PACK], BF16, name="x_grouped", align_bytes=64)
+        shared = 384
+        first, rest = offs_sb[:, : shared // LIST_ROWS], offs_sb[:, shared // LIST_ROWS :]
         for j in load_order:
             if j < 2:
                 x_bf16 = keep.tile([P, T], BF16, name="x_bf16_%d" % j)
-                nc.vector.tensor_copy(x_bf16[:], x_f32[j][:])
-                nc.scalar.activation(x_grouped[:, :, j], x_bf16[:].indirect(offs_sb[:]), ACT.Copy)
+                split = j * T // 2
+                if split:
+                    nc.scalar.copy(x_bf16[:, :split], x_f32[j][:, :split])
+                nc.vector.tensor_copy(x_bf16[:, split:], x_f32[j][:, split:])
+                nc.scalar.activation(x_grouped[:, :shared, j], x_bf16[:].indirect(first), ACT.Copy)
+                nc.vector.tensor_copy(x_grouped[:, shared:, j], x_f32[j][:].indirect(rest))
             else:
                 nc.vector.tensor_copy(x_grouped[:, :, j], x_f32[j][:].indirect(offs_sb[:]))
         x_codes = keep.tile([P, S], U32, name="x_codes", align_bytes=64)
@@ -76,7 +82,7 @@ def tile_picked_ranknet_sigmoid_lo_kernel(tc, xT, w1, offs, win, lose, out_0, ou
             nc.vector.tensor_copy(dst[:, :split], src[:, :split])
             nc.scalar.copy(dst[:, split:], src[:, split:])
 
-        deal(0, 80)
+        deal(0, 64)
         for t in range(2):
             nc.vector.quantize_mx(out=w_codes[t][:].bitcast(FP8X4), scales=w_scales[t][:], in_=w_grouped[0][:, t].rearrange("p m j -> p (m j)"))
         deal(1, 48)
@@ -111,25 +117,35 @@ def tile_picked_ranknet_sigmoid_lo_kernel(tc, xT, w1, offs, win, lose, out_0, ou
         prob = keep.tile([P, PACK, V], F32, name="prob")
         out_rows = out_0.rearrange("(p t) v -> p t v", t=PACK)
 
+        grouped = keep.tile([P, V, PACK], BF16, name="prob_grouped", align_bytes=64)
         halves = [slice(h * HALF_V, (h + 1) * HALF_V) for h in range(2)]
-        list_halves = [slice(c.start // LIST_ROWS, c.stop // LIST_ROWS) for c in halves]
+        last_pieces = [slice(0, 128), slice(128, 192), slice(192, 256)]
+
+        def entries(tile, cols):
+            return tile[:, cols.start // LIST_ROWS : cols.stop // LIST_ROWS]
+
+        def weave(copy, pair, cols):
+            copy(grouped[:, cols, 2 * pair : 2 * pair + 2], prob[:, 2 * pair : 2 * pair + 2, cols].rearrange("p t v -> p v t"))
+
         for t in range(PACK):
-            for cols, entries in zip(halves, list_halves):
-                nc.vector.tensor_copy(losers[t][:, cols], y[t][:].indirect(lose_sb[:, entries]))
-            for cols, entries in zip(halves, list_halves):
-                nc.vector.tensor_tensor(margins[t][:, cols], y[t][:].indirect(win_sb[:, entries]), losers[t][:, cols], SUB)
-            for cols in halves if t == PACK - 1 else [slice(0, V)]:
+            last = t == PACK - 1
+            for cols in halves:
+                nc.vector.tensor_copy(losers[t][:, cols], y[t][:].indirect(entries(lose_sb, cols)))
+            for cols in last_pieces if last else halves:
+                nc.vector.tensor_tensor(margins[t][:, cols], y[t][:].indirect(entries(win_sb, cols)), losers[t][:, cols], SUB)
+            for cols in last_pieces if last else [slice(0, V)]:
                 nc.scalar.activation(prob[:, t, cols], margins[t][:, cols], ACT.Sigmoid)
             nc.sync.dma_start(out_rows[:, t, :], prob[:, t, :])
+            if t == 1:
+                weave(nc.scalar.copy, 0, slice(0, V))
 
         out_codes = keep.tile([P, V], U32, name="out_codes", align_bytes=64)
         out_scales = keep.tile([P, V], U8, name="out_scales", align_bytes=64)
         words = out_1[0].rearrange("p v r -> p (v r)").bitcast(I32)
-        grouped = [keep.tile([P, HALF_V, PACK], BF16, name="prob_grouped_%d" % h, align_bytes=64) for h in range(2)]
-        for h, cols in enumerate(halves):
-            nc.vector.tensor_copy(grouped[h][:].rearrange("p (c i) t -> p c t i", i=4), prob[:, :, cols].rearrange("p t (c i) -> p c t i", i=4))
-        for h, cols in enumerate(halves):
-            nc.vector.quantize_mx(out=out_codes[:, cols].bitcast(FP8X4), scales=out_scales[:, cols], in_=grouped[h][:].rearrange("p v t -> p (v t)"))
+        for cols in last_pieces:
+            weave(nc.vector.tensor_copy, 1, cols)
+        for cols in halves:
+            nc.vector.quantize_mx(out=out_codes[:, cols].bitcast(FP8X4), scales=out_scales[:, cols], in_=grouped[:, cols].rearrange("p v t -> p (v t)"))
             nc.sync.dma_start(words[:, cols], out_codes[:, cols].bitcast(I32))
         for q, queue in enumerate((nc.scalar, nc.scalar, nc.sync, nc.sync)):
             queue.dma_start(out_2[0, 4 * q : 4 * q + 4, :].bitcast(I32), out_scales[32 * q : 32 * q + 4, :].bitcast(I32))

@@ -36,13 +36,15 @@ def tile_picked_ranknet_sigmoid_lo_kernel(tc, xT, w1, offs, win, lose, out_0, ou
 
         x_rows = xT.rearrange("(p j) t -> p j t", j=PACK)
         x_f32 = [keep.tile([P, T], F32, name="x_f32_%d" % j) for j in range(PACK)]
-        w_f32 = keep.tile([P, PACK, N], F32, name="w_f32")
+        w_f32 = [keep.tile([P, PACK, N // 2], F32, name="w_f32_%d" % h) for h in range(2)]
+        w_rows = w1.rearrange("(p j) n -> p j n", j=PACK)
         load_order = (0, 2, 1, 3)
         nc.sync.dma_start(x_f32[0][:], x_rows[:, 0, :])
         nc.sync.dma_start(offs_sb[:], offs)
         for j in load_order[1:]:
             nc.sync.dma_start(x_f32[j][:], x_rows[:, j, :])
-        nc.sync.dma_start(w_f32[:], w1.rearrange("(p j) n -> p j n", j=PACK))
+        for h in range(2):
+            nc.sync.dma_start(w_f32[h][:], w_rows[:, :, h * N // 2 : (h + 1) * N // 2])
         nc.sync.dma_start(lose_sb[:], lose)
         nc.sync.dma_start(win_sb[:], win)
 
@@ -63,29 +65,35 @@ def tile_picked_ranknet_sigmoid_lo_kernel(tc, xT, w1, offs, win, lose, out_0, ou
                 nc.vector.tensor_copy(x_bf16[:, split:], x_f32[j][:, split:])
                 nc.scalar.activation(x_grouped[:, :shared, j], x_bf16[:].indirect(first), ACT.Copy)
                 nc.vector.tensor_copy(x_grouped[:, shared:, j], x_f32[j][:].indirect(rest))
-            else:
+            elif j == 2:
                 nc.vector.tensor_copy(x_grouped[:, :, j], x_f32[j][:].indirect(offs_sb[:]))
+            else:
+                for h in range(2):
+                    nc.vector.tensor_copy(x_grouped[:, h * HALF_S : (h + 1) * HALF_S, j], x_f32[j][:].indirect(offs_sb[:, h * 16 : (h + 1) * 16]))
         x_codes = keep.tile([P, S], U32, name="x_codes", align_bytes=64)
         x_scales = keep.tile([P, S], U8, name="x_scales", align_bytes=64)
-        nc.vector.quantize_mx(out=x_codes[:].bitcast(FP8X4), scales=x_scales[:], in_=x_grouped[:].rearrange("p s j -> p (s j)"))
+        for h in range(2):
+            cols = slice(h * HALF_S, (h + 1) * HALF_S)
+            nc.vector.quantize_mx(out=x_codes[:, cols].bitcast(FP8X4), scales=x_scales[:, cols], in_=x_grouped[:, cols].rearrange("p s j -> p (s j)"))
 
-        w_dealt = w_f32[:].rearrange("p j (m t) -> p m j t", t=PACK)
+        w_dealt = [w_f32[h][:].rearrange("p j (m t) -> p m j t", t=PACK) for h in range(2)]
         w_grouped = [keep.tile([P, 2, M_TILE, PACK], BF16, name="w_grouped_%d" % pair, align_bytes=64) for pair in range(2)]
         w_codes = [keep.tile([P, M_TILE], U32, name="w_codes_%d" % t, align_bytes=64) for t in range(2)]
         w_scales = [keep.tile([P, M_TILE], U8, name="w_scales_%d" % t, align_bytes=64) for t in range(2)]
         late_codes = keep.tile([P, 2 * M_TILE], U32, name="late_codes", align_bytes=64)
         late_scales = keep.tile([P, 2 * M_TILE], U8, name="late_scales", align_bytes=64)
 
-        def deal(pair, split):
+        def deal(copy, pair, h, lo, hi):
             dst = w_grouped[pair][:].rearrange("p t m j -> p m j t")
-            src = w_dealt[:, :, :, 2 * pair : 2 * pair + 2]
-            nc.vector.tensor_copy(dst[:, :split], src[:, :split])
-            nc.scalar.copy(dst[:, split:], src[:, split:])
+            copy(dst[:, 64 * h + lo : 64 * h + hi], w_dealt[h][:, lo:hi, :, 2 * pair : 2 * pair + 2])
 
-        deal(0, 64)
+        deal(nc.scalar.copy, 0, 0, 0, 64)
+        deal(nc.scalar.copy, 1, 0, 0, 64)
+        deal(nc.vector.tensor_copy, 0, 1, 0, 40)
+        deal(nc.scalar.copy, 0, 1, 40, 64)
         for t in range(2):
             nc.vector.quantize_mx(out=w_codes[t][:].bitcast(FP8X4), scales=w_scales[t][:], in_=w_grouped[0][:, t].rearrange("p m j -> p (m j)"))
-        deal(1, 48)
+        deal(nc.scalar.copy, 1, 1, 0, 64)
         nc.vector.quantize_mx(out=late_codes[:].bitcast(FP8X4), scales=late_scales[:], in_=w_grouped[1][:].rearrange("p t m j -> p (t m j)"))
         stationary = [(w_codes[t][:], w_scales[t][:]) for t in range(2)]
         stationary = stationary + [(late_codes[:, u * M_TILE : (u + 1) * M_TILE], late_scales[:, u * M_TILE : (u + 1) * M_TILE]) for u in range(2)]
@@ -102,9 +110,9 @@ def tile_picked_ranknet_sigmoid_lo_kernel(tc, xT, w1, offs, win, lose, out_0, ou
             )
 
         y = [keep.tile([P, S], F32, name="y_%d" % t) for t in range(PACK)]
-        for h, copy in enumerate((nc.scalar.copy, nc.vector.tensor_copy)):
-            cols = slice(h * HALF_S, (h + 1) * HALF_S)
-            acc = psum.tile([P, HALF_S], F32, name="acc_0_%d" % h)
+        first_pieces = [(slice(0, 256), nc.vector.tensor_copy), (slice(256, 384), nc.scalar.copy), (slice(384, 512), nc.scalar.copy)]
+        for h, (cols, copy) in enumerate(first_pieces):
+            acc = psum.tile([P, cols.stop - cols.start], F32, name="acc_0_%d" % h)
             product(acc[:], 0, cols)
             copy(y[0][:, cols], acc[:])
         for t in range(1, PACK):
@@ -113,7 +121,6 @@ def tile_picked_ranknet_sigmoid_lo_kernel(tc, xT, w1, offs, win, lose, out_0, ou
             nc.scalar.copy(y[t][:], acc[:])
 
         losers = [keep.tile([P, V], F32, name="losers_%d" % t) for t in range(PACK)]
-        margins = [keep.tile([P, V], F32, name="margins_%d" % t) for t in range(PACK)]
         prob = keep.tile([P, PACK, V], F32, name="prob")
         out_rows = out_0.rearrange("(p t) v -> p t v", t=PACK)
 
@@ -127,22 +134,40 @@ def tile_picked_ranknet_sigmoid_lo_kernel(tc, xT, w1, offs, win, lose, out_0, ou
         def weave(copy, pair, cols):
             copy(grouped[:, cols, 2 * pair : 2 * pair + 2], prob[:, 2 * pair : 2 * pair + 2, cols].rearrange("p t v -> p v t"))
 
-        for t in range(PACK):
-            last = t == PACK - 1
+        def fetch_losers(t, cols):
+            nc.vector.tensor_copy(losers[t][:, cols], y[t][:].indirect(entries(lose_sb, cols)))
+
+        def fetch_margins(margins, t, cols):
+            nc.vector.tensor_tensor(margins[:, t % 2, cols], y[t][:].indirect(entries(win_sb, cols)), losers[t][:, cols], SUB)
+
+        whole = slice(0, V)
+        margins = keep.tile([P, 2, V], F32, name="margins_early", tag="margins")
+        for t in range(2):
             for cols in halves:
-                nc.vector.tensor_copy(losers[t][:, cols], y[t][:].indirect(entries(lose_sb, cols)))
-            for cols in last_pieces if last else halves:
-                nc.vector.tensor_tensor(margins[t][:, cols], y[t][:].indirect(entries(win_sb, cols)), losers[t][:, cols], SUB)
-            for cols in last_pieces if last else [slice(0, V)]:
-                nc.scalar.activation(prob[:, t, cols], margins[t][:, cols], ACT.Sigmoid)
+                fetch_losers(t, cols)
+            for cols in halves:
+                fetch_margins(margins, t, cols)
+            nc.scalar.activation(prob[:, t, :], margins[:, t, :], ACT.Sigmoid)
             nc.sync.dma_start(out_rows[:, t, :], prob[:, t, :])
-            if t == 1:
-                weave(nc.scalar.copy, 0, slice(0, V))
+        weave(nc.scalar.copy, 0, whole)
+        margins = keep.tile([P, 2, V], F32, name="margins_late", tag="margins")
+        fetch_losers(2, whole)
+        fetch_losers(3, whole)
+        fetch_margins(margins, 2, whole)
+        nc.scalar.activation(prob[:, 2, :], margins[:, 0, :], ACT.Sigmoid)
+        nc.sync.dma_start(out_rows[:, 2, :], prob[:, 2, :])
+        for cols in last_pieces:
+            fetch_margins(margins, 3, cols)
+        for cols in last_pieces:
+            if cols.stop == V:
+                nc.scalar.activation(grouped[:, cols, 2:4], margins[:, :, cols].rearrange("p t v -> p v t"), ACT.Sigmoid)
+            nc.scalar.activation(prob[:, 3, cols], margins[:, 1, cols], ACT.Sigmoid)
+        nc.sync.dma_start(out_rows[:, 3, :], prob[:, 3, :])
 
         out_codes = keep.tile([P, V], U32, name="out_codes", align_bytes=64)
         out_scales = keep.tile([P, V], U8, name="out_scales", align_bytes=64)
         words = out_1[0].rearrange("p v r -> p (v r)").bitcast(I32)
-        for cols in last_pieces:
+        for cols in last_pieces[:2]:
             weave(nc.vector.tensor_copy, 1, cols)
         for cols in halves:
             nc.vector.quantize_mx(out=out_codes[:, cols].bitcast(FP8X4), scales=out_scales[:, cols], in_=grouped[:, cols].rearrange("p v t -> p (v t)"))

@@ -36,15 +36,14 @@ def tile_picked_ranknet_sigmoid_lo_kernel(tc, xT, w1, offs, win, lose, out_0, ou
 
         x_rows = xT.rearrange("(p j) t -> p j t", j=PACK)
         x_f32 = [keep.tile([P, T], F32, name="x_f32_%d" % j) for j in range(PACK)]
-        w_f32 = [keep.tile([P, PACK, N // 2], F32, name="w_f32_%d" % h) for h in range(2)]
+        w_f32 = keep.tile([P, PACK, N], F32, name="w_f32")
         w_rows = w1.rearrange("(p j) n -> p j n", j=PACK)
         load_order = (0, 2, 1, 3)
         nc.sync.dma_start(x_f32[0][:], x_rows[:, 0, :])
         nc.sync.dma_start(offs_sb[:], offs)
         for j in load_order[1:]:
             nc.sync.dma_start(x_f32[j][:], x_rows[:, j, :])
-        for h in range(2):
-            nc.sync.dma_start(w_f32[h][:], w_rows[:, :, h * N // 2 : (h + 1) * N // 2])
+        nc.sync.dma_start(w_f32[:], w_rows)
         nc.sync.dma_start(lose_sb[:], lose)
         nc.sync.dma_start(win_sb[:], win)
 
@@ -76,24 +75,23 @@ def tile_picked_ranknet_sigmoid_lo_kernel(tc, xT, w1, offs, win, lose, out_0, ou
             cols = slice(h * HALF_S, (h + 1) * HALF_S)
             nc.vector.quantize_mx(out=x_codes[:, cols].bitcast(FP8X4), scales=x_scales[:, cols], in_=x_grouped[:, cols].rearrange("p s j -> p (s j)"))
 
-        w_dealt = [w_f32[h][:].rearrange("p j (m t) -> p m j t", t=PACK) for h in range(2)]
+        w_dealt = w_f32[:].rearrange("p j (m t) -> p m j t", t=PACK)
         w_grouped = [keep.tile([P, 2, M_TILE, PACK], BF16, name="w_grouped_%d" % pair, align_bytes=64) for pair in range(2)]
         w_codes = [keep.tile([P, M_TILE], U32, name="w_codes_%d" % t, align_bytes=64) for t in range(2)]
         w_scales = [keep.tile([P, M_TILE], U8, name="w_scales_%d" % t, align_bytes=64) for t in range(2)]
         late_codes = keep.tile([P, 2 * M_TILE], U32, name="late_codes", align_bytes=64)
         late_scales = keep.tile([P, 2 * M_TILE], U8, name="late_scales", align_bytes=64)
 
-        def deal(copy, pair, h, lo, hi):
+        def deal(pair, split):
             dst = w_grouped[pair][:].rearrange("p t m j -> p m j t")
-            copy(dst[:, 64 * h + lo : 64 * h + hi], w_dealt[h][:, lo:hi, :, 2 * pair : 2 * pair + 2])
+            src = w_dealt[:, :, :, 2 * pair : 2 * pair + 2]
+            nc.vector.tensor_copy(dst[:, :split], src[:, :split])
+            nc.scalar.copy(dst[:, split:], src[:, split:])
 
-        deal(nc.scalar.copy, 0, 0, 0, 64)
-        deal(nc.scalar.copy, 1, 0, 0, 64)
-        deal(nc.vector.tensor_copy, 0, 1, 0, 40)
-        deal(nc.scalar.copy, 0, 1, 40, 64)
+        deal(0, 80)
         for t in range(2):
             nc.vector.quantize_mx(out=w_codes[t][:].bitcast(FP8X4), scales=w_scales[t][:], in_=w_grouped[0][:, t].rearrange("p m j -> p (m j)"))
-        deal(nc.scalar.copy, 1, 1, 0, 64)
+        deal(1, 48)
         nc.vector.quantize_mx(out=late_codes[:].bitcast(FP8X4), scales=late_scales[:], in_=w_grouped[1][:].rearrange("p t m j -> p (t m j)"))
         stationary = [(w_codes[t][:], w_scales[t][:]) for t in range(2)]
         stationary = stationary + [(late_codes[:, u * M_TILE : (u + 1) * M_TILE], late_scales[:, u * M_TILE : (u + 1) * M_TILE]) for u in range(2)]

@@ -35,8 +35,8 @@ def tile_picked_ranknet_sigmoid_lo_kernel(tc, xT, w1, offs, win, lose, out_0, ou
         lose_sb = lists.tile([P, V // LIST_ROWS], U16, name="lose_sb")
 
         x_rows = xT.rearrange("(p j) t -> p j t", j=PACK)
-        x_f32 = [keep.tile([P, T], F32, name="x_f32_%d" % j) for j in range(PACK)]
-        w_f32 = keep.tile([P, PACK, N], F32, name="w_f32")
+        x_f32 = [keep.tile([P, T], F32, name="x_f32_%d" % j, align_bytes=256) for j in range(PACK)]
+        w_f32 = keep.tile([P, PACK, N], F32, name="w_f32", align_bytes=256)
         w_rows = w1.rearrange("(p j) n -> p j n", j=PACK)
         load_order = (0, 2, 1, 3)
         nc.sync.dma_start(x_f32[0][:], x_rows[:, 0, :])
@@ -88,10 +88,10 @@ def tile_picked_ranknet_sigmoid_lo_kernel(tc, xT, w1, offs, win, lose, out_0, ou
             nc.vector.tensor_copy(dst[:, :split], src[:, :split])
             nc.scalar.copy(dst[:, split:], src[:, split:])
 
-        deal(0, 80)
+        deal(0, 76)
         for t in range(2):
             nc.vector.quantize_mx(out=w_codes[t][:].bitcast(FP8X4), scales=w_scales[t][:], in_=w_grouped[0][:, t].rearrange("p m j -> p (m j)"))
-        deal(1, 48)
+        deal(1, 84)
         nc.vector.quantize_mx(out=late_codes[:].bitcast(FP8X4), scales=late_scales[:], in_=w_grouped[1][:].rearrange("p t m j -> p (t m j)"))
         stationary = [(w_codes[t][:], w_scales[t][:]) for t in range(2)]
         stationary = stationary + [(late_codes[:, u * M_TILE : (u + 1) * M_TILE], late_scales[:, u * M_TILE : (u + 1) * M_TILE]) for u in range(2)]
@@ -119,7 +119,7 @@ def tile_picked_ranknet_sigmoid_lo_kernel(tc, xT, w1, offs, win, lose, out_0, ou
             nc.scalar.copy(y[t][:], acc[:])
 
         losers = [keep.tile([P, V], F32, name="losers_%d" % t) for t in range(PACK)]
-        prob = keep.tile([P, PACK, V], F32, name="prob")
+        prob = keep.tile([P, PACK, V], F32, name="prob", align_bytes=256)
         out_rows = out_0.rearrange("(p t) v -> p t v", t=PACK)
 
         grouped = keep.tile([P, V, PACK], BF16, name="prob_grouped", align_bytes=64)
@@ -162,13 +162,14 @@ def tile_picked_ranknet_sigmoid_lo_kernel(tc, xT, w1, offs, win, lose, out_0, ou
             nc.scalar.activation(prob[:, 3, cols], margins[:, 1, cols], ACT.Sigmoid)
         nc.sync.dma_start(out_rows[:, 3, :], prob[:, 3, :])
 
-        out_codes = keep.tile([P, V], U32, name="out_codes", align_bytes=64)
+        out_codes = keep.tile([P, V], U32, name="out_codes", align_bytes=256)
         out_scales = keep.tile([P, V], U8, name="out_scales", align_bytes=64)
         words = out_1[0].rearrange("p v r -> p (v r)").bitcast(I32)
         for cols in last_pieces[:2]:
             weave(nc.vector.tensor_copy, 1, cols)
-        for cols in halves:
+        for cols in last_pieces:
             nc.vector.quantize_mx(out=out_codes[:, cols].bitcast(FP8X4), scales=out_scales[:, cols], in_=grouped[:, cols].rearrange("p v t -> p (v t)"))
+        for cols in halves:
             nc.sync.dma_start(words[:, cols], out_codes[:, cols].bitcast(I32))
         for q, queue in enumerate((nc.scalar, nc.scalar, nc.sync, nc.sync)):
             queue.dma_start(out_2[0, 4 * q : 4 * q + 4, :].bitcast(I32), out_scales[32 * q : 32 * q + 4, :].bitcast(I32))

@@ -156,20 +156,19 @@ def tile_picked_ranknet_sigmoid_lo_kernel(tc, xT, w1, offs, win, lose, out_0, ou
         nc.sync.dma_start(out_rows[:, 2, :], prob[:, 2, :])
         for cols in last_pieces:
             fetch_margins(margins, 3, cols)
-        for cols in last_pieces:
-            if cols.stop == V:
-                nc.scalar.activation(grouped[:, cols, 2:4], margins[:, :, cols].rearrange("p t v -> p v t"), ACT.Sigmoid)
-            nc.scalar.activation(prob[:, 3, cols], margins[:, 1, cols], ACT.Sigmoid)
-        nc.sync.dma_start(out_rows[:, 3, :], prob[:, 3, :])
+        nc.scalar.activation(prob[:, 3, halves[0]], margins[:, 1, halves[0]], ACT.Sigmoid)
+        for cols in last_pieces[1:]:
+            nc.scalar.activation(grouped[:, cols, 2:4], margins[:, :, cols].rearrange("p t v -> p v t"), ACT.Sigmoid)
+        nc.scalar.activation(prob[:, 3, halves[1]], margins[:, 1, halves[1]], ACT.Sigmoid)
+        for cols in halves:
+            nc.sync.dma_start(out_rows[:, 3, cols], prob[:, 3, cols])
 
         out_codes = keep.tile([P, V], U32, name="out_codes", align_bytes=256)
         out_scales = keep.tile([P, V], U8, name="out_scales", align_bytes=64)
         words = out_1[0].rearrange("p v r -> p (v r)").bitcast(I32)
-        for cols in last_pieces[:2]:
-            weave(nc.vector.tensor_copy, 1, cols)
-        for cols in last_pieces:
+        weave(nc.vector.tensor_copy, 1, halves[0])
+        for cols in [last_pieces[1], last_pieces[0], last_pieces[2]]:
             nc.vector.quantize_mx(out=out_codes[:, cols].bitcast(FP8X4), scales=out_scales[:, cols], in_=grouped[:, cols].rearrange("p v t -> p (v t)"))
-        for cols in halves:
-            nc.sync.dma_start(words[:, cols], out_codes[:, cols].bitcast(I32))
+        nc.sync.dma_start(words, out_codes[:].bitcast(I32))
         for q, queue in enumerate((nc.scalar, nc.scalar, nc.sync, nc.sync)):
             queue.dma_start(out_2[0, 4 * q : 4 * q + 4, :].bitcast(I32), out_scales[32 * q : 32 * q + 4, :].bitcast(I32))

@@ -62,8 +62,12 @@ def tile_picked_ranknet_sigmoid_lo_kernel(tc, xT, w1, offs, win, lose, out_0, ou
                 if split:
                     nc.scalar.copy(x_bf16[:, :split], x_f32[j][:, :split])
                 nc.vector.tensor_copy(x_bf16[:, split:], x_f32[j][:, split:])
-                nc.scalar.activation(x_grouped[:, :shared, j], x_bf16[:].indirect(first), ACT.Copy)
-                nc.vector.tensor_copy(x_grouped[:, shared:, j], x_f32[j][:].indirect(rest))
+                if j == 0:
+                    nc.scalar.activation(x_grouped[:, :shared, j], x_bf16[:].indirect(first), ACT.Copy)
+                    nc.vector.tensor_copy(x_grouped[:, shared:, j], x_f32[j][:].indirect(rest))
+                else:
+                    for h in range(2):
+                        nc.scalar.activation(x_grouped[:, h * HALF_S : (h + 1) * HALF_S, j], x_bf16[:].indirect(offs_sb[:, h * 16 : (h + 1) * 16]), ACT.Copy)
             elif j == 2:
                 nc.vector.tensor_copy(x_grouped[:, :, j], x_f32[j][:].indirect(offs_sb[:]))
             else:

@@ -117,12 +117,17 @@ def tile_picked_ranknet_sigmoid_lo_kernel(tc, xT, w1, offs, win, lose, out_0, ou
             acc = psum.tile([P, cols.stop - cols.start], F32, name="acc_0_%d" % h)
             product(acc[:], 0, cols)
             copy(y[0][:, cols], acc[:])
-        for t in range(1, PACK):
+        second_pieces = [(slice(0, 128), nc.vector.tensor_copy), (slice(128, 256), nc.scalar.copy), (slice(256, 512), nc.scalar.copy)]
+        for h, (cols, copy) in enumerate(second_pieces):
+            acc = psum.tile([P, cols.stop - cols.start], F32, name="acc_1_%d" % h)
+            product(acc[:], 1, cols)
+            copy(y[1][:, cols], acc[:])
+        for t in range(2, PACK):
             acc = psum.tile([P, S], F32, name="acc_%d" % t)
             product(acc[:], t, slice(0, S))
             nc.scalar.copy(y[t][:], acc[:])
 
-        losers = [keep.tile([P, V], F32, name="losers_%d" % t) for t in range(PACK)]
+        losers = [keep.tile([P, V], F32, name="losers_%d" % t, tag="losers_%d" % (t % 2)) for t in range(PACK)]
         prob = keep.tile([P, PACK, V], F32, name="prob", align_bytes=256)
         out_rows = out_0.rearrange("(p t) v -> p t v", t=PACK)
 
@@ -143,16 +148,15 @@ def tile_picked_ranknet_sigmoid_lo_kernel(tc, xT, w1, offs, win, lose, out_0, ou
             nc.vector.tensor_tensor(margins[:, t % 2, cols], y[t][:].indirect(entries(win_sb, cols)), losers[t][:, cols], SUB)
 
         whole = slice(0, V)
-        margins = keep.tile([P, 2, V], F32, name="margins_early", tag="margins")
+        margins = keep.tile([P, 2, V], F32, name="margins_early", tag="margins", align_bytes=64)
         for t in range(2):
-            for cols in halves:
-                fetch_losers(t, cols)
-            for cols in halves:
-                fetch_margins(margins, t, cols)
+            fetch_losers(t, whole)
+        for t in range(2):
+            fetch_margins(margins, t, whole)
             nc.scalar.activation(prob[:, t, :], margins[:, t, :], ACT.Sigmoid)
             nc.sync.dma_start(out_rows[:, t, :], prob[:, t, :])
         weave(nc.scalar.copy, 0, whole)
-        margins = keep.tile([P, 2, V], F32, name="margins_late", tag="margins")
+        margins = keep.tile([P, 2, V], F32, name="margins_late", tag="margins", align_bytes=64)
         fetch_losers(2, whole)
         fetch_losers(3, whole)
         fetch_margins(margins, 2, whole)
@@ -164,8 +168,8 @@ def tile_picked_ranknet_sigmoid_lo_kernel(tc, xT, w1, offs, win, lose, out_0, ou
         for cols in last_pieces[1:]:
             nc.scalar.activation(grouped[:, cols, 2:4], margins[:, :, cols].rearrange("p t v -> p v t"), ACT.Sigmoid)
         nc.scalar.activation(prob[:, 3, halves[1]], margins[:, 1, halves[1]], ACT.Sigmoid)
-        for cols in halves:
-            nc.sync.dma_start(out_rows[:, 3, cols], prob[:, 3, cols])
+        for cols, queue in zip(halves, (nc.sync, nc.scalar)):
+            queue.dma_start(out_rows[:, 3, cols], prob[:, 3, cols])
 
         out_codes = keep.tile([P, V], U32, name="out_codes", align_bytes=256)
         out_scales = keep.tile([P, V], U8, name="out_scales", align_bytes=64)

@@ -168,8 +168,8 @@ def tile_picked_ranknet_sigmoid_lo_kernel(tc, xT, w1, offs, win, lose, out_0, ou
         for cols in last_pieces[1:]:
             nc.scalar.activation(grouped[:, cols, 2:4], margins[:, :, cols].rearrange("p t v -> p v t"), ACT.Sigmoid)
         nc.scalar.activation(prob[:, 3, halves[1]], margins[:, 1, halves[1]], ACT.Sigmoid)
-        for cols, queue in zip(halves, (nc.sync, nc.scalar)):
-            queue.dma_start(out_rows[:, 3, cols], prob[:, 3, cols])
+        for cols in halves:
+            nc.sync.dma_start(out_rows[:, 3, cols], prob[:, 3, cols])
 
         out_codes = keep.tile([P, V], U32, name="out_codes", align_bytes=256)
         out_scales = keep.tile([P, V], U8, name="out_scales", align_bytes=64)

@@ -112,22 +112,16 @@ def tile_picked_ranknet_sigmoid_lo_kernel(tc, xT, w1, offs, win, lose, out_0, ou
             )
 
         y = [keep.tile([P, S], F32, name="y_%d" % t) for t in range(PACK)]
-        first_pieces = [(slice(0, 256), nc.vector.tensor_copy), (slice(256, 384), nc.scalar.copy), (slice(384, 512), nc.scalar.copy)]
-        for h, (cols, copy) in enumerate(first_pieces):
-            acc = psum.tile([P, cols.stop - cols.start], F32, name="acc_0_%d" % h)
-            product(acc[:], 0, cols)
-            copy(y[0][:, cols], acc[:])
-        second_pieces = [(slice(0, 128), nc.vector.tensor_copy), (slice(128, 256), nc.scalar.copy), (slice(256, 512), nc.scalar.copy)]
-        for h, (cols, copy) in enumerate(second_pieces):
-            acc = psum.tile([P, cols.stop - cols.start], F32, name="acc_1_%d" % h)
-            product(acc[:], 1, cols)
-            copy(y[1][:, cols], acc[:])
-        for t in range(2, PACK):
-            acc = psum.tile([P, S], F32, name="acc_%d" % t)
-            product(acc[:], t, slice(0, S))
-            nc.scalar.copy(y[t][:], acc[:])
 
-        losers = [keep.tile([P, V], F32, name="losers_%d" % t, tag="losers_%d" % (t % 2)) for t in range(PACK)]
+        def scores(t, pieces):
+            for h, (cols, copy, bank) in enumerate(pieces):
+                acc = psum.tile([P, cols.stop - cols.start], F32, name="acc_%d_%d" % (t, h), tag="bank_%d" % bank)
+                product(acc[:], t, cols)
+                copy(y[t][:, cols], acc[:])
+
+        front, back = slice(0, HALF_S), slice(HALF_S, S)
+
+        losers = [keep.tile([P, V], F32, name="losers_%d" % t, tag="losers_%d" % t) for t in range(PACK)]
         prob = keep.tile([P, PACK, V], F32, name="prob", align_bytes=256)
         out_rows = out_0.rearrange("(p t) v -> p t v", t=PACK)
 
@@ -141,24 +135,28 @@ def tile_picked_ranknet_sigmoid_lo_kernel(tc, xT, w1, offs, win, lose, out_0, ou
         def weave(copy, pair, cols):
             copy(grouped[:, cols, 2 * pair : 2 * pair + 2], prob[:, 2 * pair : 2 * pair + 2, cols].rearrange("p t v -> p v t"))
 
-        def fetch_losers(t, cols):
-            nc.vector.tensor_copy(losers[t][:, cols], y[t][:].indirect(entries(lose_sb, cols)))
+        def fetch_losers_scalar(t, cols):
+            nc.scalar.activation(losers[t][:, cols], y[t][:].indirect(entries(lose_sb, cols)), ACT.Copy)
 
         def fetch_margins(margins, t, cols):
             nc.vector.tensor_tensor(margins[:, t % 2, cols], y[t][:].indirect(entries(win_sb, cols)), losers[t][:, cols], SUB)
 
         whole = slice(0, V)
-        margins = keep.tile([P, 2, V], F32, name="margins_early", tag="margins", align_bytes=64)
+        margins = keep.tile([P, 2, V], F32, name="margins_early", align_bytes=64)
+        scores(0, [(slice(0, 256), nc.vector.tensor_copy, 0), (slice(256, 384), nc.scalar.copy, 1), (slice(384, 512), nc.scalar.copy, 2)])
+        scores(1, [(front, nc.vector.tensor_copy, 3), (back, nc.vector.tensor_copy, 4)])
+        fetch_losers_scalar(0, whole)
+        scores(2, [(front, nc.vector.tensor_copy, 5), (back, nc.vector.tensor_copy, 6)])
+        fetch_losers_scalar(1, whole)
+        scores(3, [(front, nc.vector.tensor_copy, 7), (back, nc.scalar.copy, 4)])
+        fetch_margins(margins, 0, whole)
+        fetch_losers_scalar(2, whole)
+        fetch_losers_scalar(3, whole)
+        fetch_margins(margins, 1, whole)
         for t in range(2):
-            fetch_losers(t, whole)
-        for t in range(2):
-            fetch_margins(margins, t, whole)
             nc.scalar.activation(prob[:, t, :], margins[:, t, :], ACT.Sigmoid)
             nc.sync.dma_start(out_rows[:, t, :], prob[:, t, :])
-        weave(nc.scalar.copy, 0, whole)
-        margins = keep.tile([P, 2, V], F32, name="margins_late", tag="margins", align_bytes=64)
-        fetch_losers(2, whole)
-        fetch_losers(3, whole)
+        margins = keep.tile([P, 2, V], F32, name="margins_late", align_bytes=64)
         fetch_margins(margins, 2, whole)
         nc.scalar.activation(prob[:, 2, :], margins[:, 0, :], ACT.Sigmoid)
         nc.sync.dma_start(out_rows[:, 2, :], prob[:, 2, :])
@@ -174,6 +172,7 @@ def tile_picked_ranknet_sigmoid_lo_kernel(tc, xT, w1, offs, win, lose, out_0, ou
         out_codes = keep.tile([P, V], U32, name="out_codes", align_bytes=256)
         out_scales = keep.tile([P, V], U8, name="out_scales", align_bytes=64)
         words = out_1[0].rearrange("p v r -> p (v r)").bitcast(I32)
+        weave(nc.vector.tensor_copy, 0, whole)
         weave(nc.vector.tensor_copy, 1, halves[0])
         for cols in [last_pieces[1], last_pieces[0], last_pieces[2]]:
             nc.vector.quantize_mx(out=out_codes[:, cols].bitcast(FP8X4), scales=out_scales[:, cols], in_=grouped[:, cols].rearrange("p v t -> p (v t)"))

@@ -38,7 +38,7 @@ def tile_picked_ranknet_sigmoid_lo_kernel(tc, xT, w1, offs, win, lose, out_0, ou
         x_f32 = [keep.tile([P, T], F32, name="x_f32_%d" % j, align_bytes=256) for j in range(PACK)]
         w_f32 = keep.tile([P, PACK, N], F32, name="w_f32", align_bytes=256)
         w_rows = w1.rearrange("(p j) n -> p j n", j=PACK)
-        load_order = (0, 2, 1, 3)
+        load_order = (0, 1, 2, 3)
         nc.sync.dma_start(x_f32[0][:], x_rows[:, 0, :])
         nc.sync.dma_start(offs_sb[:], offs)
         for j in load_order[1:]:
@@ -52,31 +52,22 @@ def tile_picked_ranknet_sigmoid_lo_kernel(tc, xT, w1, offs, win, lose, out_0, ou
         nc.vector.memset(warm_in[:], 0.0)
         nc.scalar.activation(warm_out[:], warm_in[:], ACT.Sigmoid)
 
+        def entries(tile, cols):
+            return tile[:, cols.start // LIST_ROWS : cols.stop // LIST_ROWS]
+
         x_grouped = keep.tile([P, S, PACK], BF16, name="x_grouped", align_bytes=64)
-        shared = 384
-        first, rest = offs_sb[:, : shared // LIST_ROWS], offs_sb[:, shared // LIST_ROWS :]
-        for j in load_order:
-            if j < 2:
-                x_bf16 = keep.tile([P, T], BF16, name="x_bf16_%d" % j)
-                split = j * T // 2
-                if split:
-                    nc.scalar.copy(x_bf16[:, :split], x_f32[j][:, :split])
-                nc.vector.tensor_copy(x_bf16[:, split:], x_f32[j][:, split:])
-                if j == 0:
-                    nc.scalar.activation(x_grouped[:, :shared, j], x_bf16[:].indirect(first), ACT.Copy)
-                    nc.vector.tensor_copy(x_grouped[:, shared:, j], x_f32[j][:].indirect(rest))
-                else:
-                    for h in range(2):
-                        nc.scalar.activation(x_grouped[:, h * HALF_S : (h + 1) * HALF_S, j], x_bf16[:].indirect(offs_sb[:, h * 16 : (h + 1) * 16]), ACT.Copy)
-            elif j == 2:
-                nc.vector.tensor_copy(x_grouped[:, :, j], x_f32[j][:].indirect(offs_sb[:]))
-            else:
-                for h in range(2):
-                    nc.vector.tensor_copy(x_grouped[:, h * HALF_S : (h + 1) * HALF_S, j], x_f32[j][:].indirect(offs_sb[:, h * 16 : (h + 1) * 16]))
+        shared = 320
+        picked = [keep.tile([P, 2, S - shared], BF16, name="picked_%d" % pair) for pair in range(2)]
+        for j in range(PACK):
+            pieces = [slice(0, shared)] if j < PACK - 1 else [slice(0, 192), slice(192, shared)]
+            for cols in pieces:
+                nc.vector.tensor_copy(x_grouped[:, cols, j], x_f32[j][:].indirect(entries(offs_sb, cols)))
+            nc.scalar.activation(picked[j // 2][:, j % 2, :], x_f32[j][:].indirect(entries(offs_sb, slice(shared, S))), ACT.Copy)
+            if j % 2:
+                nc.scalar.copy(x_grouped[:, shared:, j - 1 : j + 1], picked[j // 2][:].rearrange("p j s -> p s j"))
         x_codes = keep.tile([P, S], U32, name="x_codes", align_bytes=64)
         x_scales = keep.tile([P, S], U8, name="x_scales", align_bytes=64)
-        for h in range(2):
-            cols = slice(h * HALF_S, (h + 1) * HALF_S)
+        for cols in (slice(0, 128), slice(128, 256), slice(256, 512)):
             nc.vector.quantize_mx(out=x_codes[:, cols].bitcast(FP8X4), scales=x_scales[:, cols], in_=x_grouped[:, cols].rearrange("p s j -> p (s j)"))
 
         w_dealt = w_f32[:].rearrange("p j (m t) -> p m j t", t=PACK)
@@ -128,9 +119,6 @@ def tile_picked_ranknet_sigmoid_lo_kernel(tc, xT, w1, offs, win, lose, out_0, ou
         grouped = keep.tile([P, V, PACK], BF16, name="prob_grouped", align_bytes=64)
         halves = [slice(h * HALF_V, (h + 1) * HALF_V) for h in range(2)]
         last_pieces = [slice(0, 128), slice(128, 192), slice(192, 256)]
-
-        def entries(tile, cols):
-            return tile[:, cols.start // LIST_ROWS : cols.stop // LIST_ROWS]
 
         def weave(copy, pair, cols):
             copy(grouped[:, cols, 2 * pair : 2 * pair + 2], prob[:, 2 * pair : 2 * pair + 2, cols].rearrange("p t v -> p v t"))

@@ -114,23 +114,19 @@ def tile_picked_ranknet_sigmoid_lo_kernel(tc, xT, w1, offs, win, lose, out_0, ou
 
         losers = [keep.tile([P, V], F32, name="losers_%d" % t, tag="losers_%d" % t) for t in range(PACK)]
         prob = keep.tile([P, PACK, V], F32, name="prob", align_bytes=256)
-        out_rows = out_0.rearrange("(p t) v -> p t v", t=PACK)
 
         grouped = keep.tile([P, V, PACK], BF16, name="prob_grouped", align_bytes=64)
         halves = [slice(h * HALF_V, (h + 1) * HALF_V) for h in range(2)]
         last_pieces = [slice(0, 128), slice(128, 192), slice(192, 256)]
 
-        def weave(copy, pair, cols):
-            copy(grouped[:, cols, 2 * pair : 2 * pair + 2], prob[:, 2 * pair : 2 * pair + 2, cols].rearrange("p t v -> p v t"))
-
         def fetch_losers_scalar(t, cols):
             nc.scalar.activation(losers[t][:, cols], y[t][:].indirect(entries(lose_sb, cols)), ACT.Copy)
 
         def fetch_margins(margins, t, cols):
-            nc.vector.tensor_tensor(margins[:, t % 2, cols], y[t][:].indirect(entries(win_sb, cols)), losers[t][:, cols], SUB)
+            nc.vector.tensor_tensor(margins[:, t, cols], y[t][:].indirect(entries(win_sb, cols)), losers[t][:, cols], SUB)
 
         whole = slice(0, V)
-        margins = keep.tile([P, 2, V], F32, name="margins_early", align_bytes=64)
+        margins = keep.tile([P, PACK, V], F32, name="margins", align_bytes=64)
         scores(0, [(slice(0, 256), nc.vector.tensor_copy, 0), (slice(256, 384), nc.scalar.copy, 1), (slice(384, 512), nc.scalar.copy, 2)])
         scores(1, [(front, nc.vector.tensor_copy, 3), (back, nc.vector.tensor_copy, 4)])
         fetch_losers_scalar(0, whole)
@@ -141,27 +137,29 @@ def tile_picked_ranknet_sigmoid_lo_kernel(tc, xT, w1, offs, win, lose, out_0, ou
         fetch_losers_scalar(2, whole)
         fetch_losers_scalar(3, whole)
         fetch_margins(margins, 1, whole)
-        for t in range(2):
-            nc.scalar.activation(prob[:, t, :], margins[:, t, :], ACT.Sigmoid)
-            nc.sync.dma_start(out_rows[:, t, :], prob[:, t, :])
-        margins = keep.tile([P, 2, V], F32, name="margins_late", align_bytes=64)
+        out_flat = out_0.rearrange("(p t) v -> p (t v)", t=PACK)
+        prob_flat = prob[:].rearrange("p t v -> p (t v)")
+
+        def store(start, stop):
+            nc.sync.dma_start(out_flat[:, start:stop], prob_flat[:, start:stop])
+
+        nc.scalar.activation(prob[:, 0:2, :], margins[:, 0:2, :], ACT.Sigmoid)
+        store(0, 2 * V)
         fetch_margins(margins, 2, whole)
-        nc.scalar.activation(prob[:, 2, :], margins[:, 0, :], ACT.Sigmoid)
-        nc.sync.dma_start(out_rows[:, 2, :], prob[:, 2, :])
+        nc.scalar.activation(prob[:, 2, :], margins[:, 2, :], ACT.Sigmoid)
         for cols in last_pieces:
             fetch_margins(margins, 3, cols)
-        nc.scalar.activation(prob[:, 3, halves[0]], margins[:, 1, halves[0]], ACT.Sigmoid)
+        nc.scalar.activation(prob[:, 3, halves[0]], margins[:, 3, halves[0]], ACT.Sigmoid)
+        store(2 * V, 3 * V + HALF_V)
         for cols in last_pieces[1:]:
-            nc.scalar.activation(grouped[:, cols, 2:4], margins[:, :, cols].rearrange("p t v -> p v t"), ACT.Sigmoid)
-        nc.scalar.activation(prob[:, 3, halves[1]], margins[:, 1, halves[1]], ACT.Sigmoid)
-        for cols in halves:
-            nc.sync.dma_start(out_rows[:, 3, cols], prob[:, 3, cols])
+            nc.scalar.activation(grouped[:, cols, :], margins[:, :, cols].rearrange("p t v -> p v t"), ACT.Sigmoid)
+        nc.scalar.activation(prob[:, 3, halves[1]], margins[:, 3, halves[1]], ACT.Sigmoid)
+        store(3 * V + HALF_V, 4 * V)
 
         out_codes = keep.tile([P, V], U32, name="out_codes", align_bytes=256)
         out_scales = keep.tile([P, V], U8, name="out_scales", align_bytes=64)
         words = out_1[0].rearrange("p v r -> p (v r)").bitcast(I32)
-        weave(nc.vector.tensor_copy, 0, whole)
-        weave(nc.vector.tensor_copy, 1, halves[0])
+        nc.vector.tensor_copy(grouped[:, halves[0], :], prob[:, :, halves[0]].rearrange("p t v -> p v t"))
         for cols in [last_pieces[1], last_pieces[0], last_pieces[2]]:
             nc.vector.quantize_mx(out=out_codes[:, cols].bitcast(FP8X4), scales=out_scales[:, cols], in_=grouped[:, cols].rearrange("p v t -> p (v t)"))
         nc.sync.dma_start(words, out_codes[:].bitcast(I32))

@@ -125,6 +125,9 @@ def tile_picked_ranknet_sigmoid_lo_kernel(tc, xT, w1, offs, win, lose, out_0, ou
         def fetch_margins(margins, t, cols):
             nc.vector.tensor_tensor(margins[:, t, cols], y[t][:].indirect(entries(win_sb, cols)), losers[t][:, cols], SUB)
 
+        def by_twos(view, pattern):
+            return view.rearrange(pattern, i=2)
+
         whole = slice(0, V)
         margins = keep.tile([P, PACK, V], F32, name="margins", align_bytes=64)
         scores(0, [(slice(0, 256), nc.vector.tensor_copy, 0), (slice(256, 384), nc.scalar.copy, 1), (slice(384, 512), nc.scalar.copy, 2)])
@@ -152,14 +155,14 @@ def tile_picked_ranknet_sigmoid_lo_kernel(tc, xT, w1, offs, win, lose, out_0, ou
         nc.scalar.activation(prob[:, 3, halves[0]], margins[:, 3, halves[0]], ACT.Sigmoid)
         store(2 * V, 3 * V + HALF_V)
         for cols in last_pieces[1:]:
-            nc.scalar.activation(grouped[:, cols, :], margins[:, :, cols].rearrange("p t v -> p v t"), ACT.Sigmoid)
+            nc.scalar.activation(by_twos(grouped[:, cols, :], "p (c i) t -> p c t i"), by_twos(margins[:, :, cols], "p t (c i) -> p c t i"), ACT.Sigmoid)
         nc.scalar.activation(prob[:, 3, halves[1]], margins[:, 3, halves[1]], ACT.Sigmoid)
         store(3 * V + HALF_V, 4 * V)
 
         out_codes = keep.tile([P, V], U32, name="out_codes", align_bytes=256)
         out_scales = keep.tile([P, V], U8, name="out_scales", align_bytes=64)
         words = out_1[0].rearrange("p v r -> p (v r)").bitcast(I32)
-        nc.vector.tensor_copy(grouped[:, halves[0], :], prob[:, :, halves[0]].rearrange("p t v -> p v t"))
+        nc.vector.tensor_copy(by_twos(grouped[:, halves[0], :], "p (c i) t -> p c t i"), by_twos(prob[:, :, halves[0]], "p t (c i) -> p c t i"))
         for cols in [last_pieces[1], last_pieces[0], last_pieces[2]]:
             nc.vector.quantize_mx(out=out_codes[:, cols].bitcast(FP8X4), scales=out_scales[:, cols], in_=grouped[:, cols].rearrange("p v t -> p (v t)"))
         nc.sync.dma_start(words, out_codes[:].bitcast(I32))

@@ -36,14 +36,16 @@ def tile_picked_ranknet_sigmoid_lo_kernel(tc, xT, w1, offs, win, lose, out_0, ou
 
         x_rows = xT.rearrange("(p j) t -> p j t", j=PACK)
         x_f32 = [keep.tile([P, T], F32, name="x_f32_%d" % j, align_bytes=256) for j in range(PACK)]
-        w_f32 = keep.tile([P, PACK, N], F32, name="w_f32", align_bytes=256)
-        w_rows = w1.rearrange("(p j) n -> p j n", j=PACK)
+        w_f32 = keep.tile([P, PACK * N], F32, name="w_f32", align_bytes=256)
+        w_rows = w1.rearrange("(p j) n -> p (j n)", j=PACK)
+        early = PACK * N - N // 2
         load_order = (0, 1, 2, 3)
         nc.sync.dma_start(x_f32[0][:], x_rows[:, 0, :])
         nc.sync.dma_start(offs_sb[:], offs)
         for j in load_order[1:]:
             nc.sync.dma_start(x_f32[j][:], x_rows[:, j, :])
-        nc.sync.dma_start(w_f32[:], w_rows)
+        nc.sync.dma_start(w_f32[:, :early], w_rows[:, :early])
+        nc.sync.dma_start(w_f32[:, early:], w_rows[:, early:])
         nc.sync.dma_start(lose_sb[:], lose)
         nc.sync.dma_start(win_sb[:], win)
 
@@ -56,9 +58,10 @@ def tile_picked_ranknet_sigmoid_lo_kernel(tc, xT, w1, offs, win, lose, out_0, ou
             return tile[:, cols.start // LIST_ROWS : cols.stop // LIST_ROWS]
 
         x_grouped = keep.tile([P, S, PACK], BF16, name="x_grouped", align_bytes=64)
-        shared = 320
-        picked = [keep.tile([P, 2, S - shared], BF16, name="picked_%d" % pair) for pair in range(2)]
+        shares = (320, 352)
+        picked = [keep.tile([P, 2, S - shares[pair]], BF16, name="picked_%d" % pair) for pair in range(2)]
         for j in range(PACK):
+            shared = shares[j // 2]
             pieces = [slice(0, shared)] if j < PACK - 1 else [slice(0, 192), slice(192, shared)]
             for cols in pieces:
                 nc.vector.tensor_copy(x_grouped[:, cols, j], x_f32[j][:].indirect(entries(offs_sb, cols)))
@@ -70,23 +73,24 @@ def tile_picked_ranknet_sigmoid_lo_kernel(tc, xT, w1, offs, win, lose, out_0, ou
         for cols in (slice(0, 128), slice(128, 256), slice(256, 512)):
             nc.vector.quantize_mx(out=x_codes[:, cols].bitcast(FP8X4), scales=x_scales[:, cols], in_=x_grouped[:, cols].rearrange("p s j -> p (s j)"))
 
-        w_dealt = w_f32[:].rearrange("p j (m t) -> p m j t", t=PACK)
+        w_dealt = w_f32[:].rearrange("p (j m t) -> p m j t", j=PACK, t=PACK)
         w_grouped = [keep.tile([P, 2, M_TILE, PACK], BF16, name="w_grouped_%d" % pair, align_bytes=64) for pair in range(2)]
         w_codes = [keep.tile([P, M_TILE], U32, name="w_codes_%d" % t, align_bytes=64) for t in range(2)]
         w_scales = [keep.tile([P, M_TILE], U8, name="w_scales_%d" % t, align_bytes=64) for t in range(2)]
         late_codes = keep.tile([P, 2 * M_TILE], U32, name="late_codes", align_bytes=64)
         late_scales = keep.tile([P, 2 * M_TILE], U8, name="late_scales", align_bytes=64)
 
-        def deal(pair, split):
+        def deal(pair, start, split, stop):
             dst = w_grouped[pair][:].rearrange("p t m j -> p m j t")
             src = w_dealt[:, :, :, 2 * pair : 2 * pair + 2]
-            nc.vector.tensor_copy(dst[:, :split], src[:, :split])
-            nc.scalar.copy(dst[:, split:], src[:, split:])
+            nc.vector.tensor_copy(dst[:, start:split], src[:, start:split])
+            nc.scalar.copy(dst[:, split:stop], src[:, split:stop])
 
-        deal(0, 76)
+        deal(0, 0, 38, 64)
+        deal(0, 64, 102, 128)
         for t in range(2):
             nc.vector.quantize_mx(out=w_codes[t][:].bitcast(FP8X4), scales=w_scales[t][:], in_=w_grouped[0][:, t].rearrange("p m j -> p (m j)"))
-        deal(1, 84)
+        deal(1, 0, 76, 128)
         nc.vector.quantize_mx(out=late_codes[:].bitcast(FP8X4), scales=late_scales[:], in_=w_grouped[1][:].rearrange("p t m j -> p (t m j)"))
         stationary = [(w_codes[t][:], w_scales[t][:]) for t in range(2)]
         stationary = stationary + [(late_codes[:, u * M_TILE : (u + 1) * M_TILE], late_scales[:, u * M_TILE : (u + 1) * M_TILE]) for u in range(2)]
@@ -146,8 +150,9 @@ def tile_picked_ranknet_sigmoid_lo_kernel(tc, xT, w1, offs, win, lose, out_0, ou
         def store(start, stop):
             nc.sync.dma_start(out_flat[:, start:stop], prob_flat[:, start:stop])
 
-        nc.scalar.activation(prob[:, 0:2, :], margins[:, 0:2, :], ACT.Sigmoid)
-        store(0, 2 * V)
+        for t in range(2):
+            nc.scalar.activation(prob[:, t, :], margins[:, t, :], ACT.Sigmoid)
+            store(t * V, (t + 1) * V)
         fetch_margins(margins, 2, whole)
         nc.scalar.activation(prob[:, 2, :], margins[:, 2, :], ACT.Sigmoid)
         for cols in last_pieces:

@@ -150,25 +150,24 @@ def tile_picked_ranknet_sigmoid_lo_kernel(tc, xT, w1, offs, win, lose, out_0, ou
         def store(start, stop):
             nc.sync.dma_start(out_flat[:, start:stop], prob_flat[:, start:stop])
 
-        for t in range(2):
-            nc.scalar.activation(prob[:, t, :], margins[:, t, :], ACT.Sigmoid)
-            store(t * V, (t + 1) * V)
+        nc.scalar.activation(prob[:, 0:2, :], margins[:, 0:2, :], ACT.Sigmoid)
         fetch_margins(margins, 2, whole)
         nc.scalar.activation(prob[:, 2, :], margins[:, 2, :], ACT.Sigmoid)
+        store(0, 3 * V)
         for cols in last_pieces:
             fetch_margins(margins, 3, cols)
         nc.scalar.activation(prob[:, 3, halves[0]], margins[:, 3, halves[0]], ACT.Sigmoid)
-        store(2 * V, 3 * V + HALF_V)
-        for cols in last_pieces[1:]:
-            nc.scalar.activation(by_twos(grouped[:, cols, :], "p (c i) t -> p c t i"), by_twos(margins[:, :, cols], "p t (c i) -> p c t i"), ACT.Sigmoid)
-        nc.scalar.activation(prob[:, 3, halves[1]], margins[:, 3, halves[1]], ACT.Sigmoid)
-        store(3 * V + HALF_V, 4 * V)
+        nc.scalar.activation(prob[:, 3, last_pieces[1]], margins[:, 3, last_pieces[1]], ACT.Sigmoid)
+        nc.scalar.activation(by_twos(grouped[:, last_pieces[2], :], "p (c i) t -> p c t i"), by_twos(margins[:, :, last_pieces[2]], "p t (c i) -> p c t i"), ACT.Sigmoid)
+        nc.scalar.activation(prob[:, 3, last_pieces[2]], margins[:, 3, last_pieces[2]], ACT.Sigmoid)
+        store(3 * V, 4 * V)
 
         out_codes = keep.tile([P, V], U32, name="out_codes", align_bytes=256)
         out_scales = keep.tile([P, V], U8, name="out_scales", align_bytes=64)
         words = out_1[0].rearrange("p v r -> p (v r)").bitcast(I32)
-        nc.vector.tensor_copy(by_twos(grouped[:, halves[0], :], "p (c i) t -> p c t i"), by_twos(prob[:, :, halves[0]], "p t (c i) -> p c t i"))
-        for cols in [last_pieces[1], last_pieces[0], last_pieces[2]]:
+        for cols in last_pieces[:2]:
+            nc.vector.tensor_copy(by_twos(grouped[:, cols, :], "p (c i) t -> p c t i"), by_twos(prob[:, :, cols], "p t (c i) -> p c t i"))
+        for cols in last_pieces:
             nc.vector.quantize_mx(out=out_codes[:, cols].bitcast(FP8X4), scales=out_scales[:, cols], in_=grouped[:, cols].rearrange("p v t -> p (v t)"))
         nc.sync.dma_start(words, out_codes[:].bitcast(I32))
         for q, queue in enumerate((nc.scalar, nc.scalar, nc.sync, nc.sync)):

@@ -45,8 +45,8 @@ def tile_picked_ranknet_sigmoid_lo_kernel(tc, xT, w1, offs, win, lose, out_0, ou
         for j in load_order[1:]:
             nc.sync.dma_start(x_f32[j][:], x_rows[:, j, :])
         nc.sync.dma_start(w_f32[:, :early], w_rows[:, :early])
-        nc.sync.dma_start(w_f32[:, early:], w_rows[:, early:])
         nc.sync.dma_start(lose_sb[:], lose)
+        nc.sync.dma_start(w_f32[:, early:], w_rows[:, early:])
         nc.sync.dma_start(win_sb[:], win)
 
         warm_in = keep.tile([P, 1], F32, name="warm_in")

@@ -58,19 +58,29 @@ def tile_picked_ranknet_sigmoid_lo_kernel(tc, xT, w1, offs, win, lose, out_0, ou
             return tile[:, cols.start // LIST_ROWS : cols.stop // LIST_ROWS]
 
         x_grouped = keep.tile([P, S, PACK], BF16, name="x_grouped", align_bytes=64)
-        shares = (320, 352)
-        picked = [keep.tile([P, 2, S - shares[pair]], BF16, name="picked_%d" % pair) for pair in range(2)]
+        shared = 320
+        picked = keep.tile([P, PACK, S - shared], BF16, name="picked")
+
+        def pick(j, cols):
+            nc.scalar.activation(picked[:, j, cols.start - shared : cols.stop - shared], x_f32[j][:].indirect(entries(offs_sb, cols)), ACT.Copy)
+
+        def lay_in(cols):
+            src = picked[:, :, cols.start - shared : cols.stop - shared]
+            nc.scalar.copy(x_grouped[:, cols, :].rearrange("p (c i) j -> p c j i", i=2), src.rearrange("p j (c i) -> p c j i", i=2))
+
         for j in range(PACK):
-            shared = shares[j // 2]
-            pieces = [slice(0, shared)] if j < PACK - 1 else [slice(0, 192), slice(192, shared)]
-            for cols in pieces:
+            for cols in [slice(0, shared)] if j < PACK - 1 else [slice(0, 192), slice(192, shared)]:
                 nc.vector.tensor_copy(x_grouped[:, cols, j], x_f32[j][:].indirect(entries(offs_sb, cols)))
-            nc.scalar.activation(picked[j // 2][:, j % 2, :], x_f32[j][:].indirect(entries(offs_sb, slice(shared, S))), ACT.Copy)
-            if j % 2:
-                nc.scalar.copy(x_grouped[:, shared:, j - 1 : j + 1], picked[j // 2][:].rearrange("p j s -> p s j"))
+        rest_pieces = [slice(shared, 384), slice(384, S)]
+        for j in range(PACK - 1):
+            pick(j, slice(shared, S))
+        for cols in rest_pieces:
+            pick(PACK - 1, cols)
+        for cols in rest_pieces:
+            lay_in(cols)
         x_codes = keep.tile([P, S], U32, name="x_codes", align_bytes=64)
         x_scales = keep.tile([P, S], U8, name="x_scales", align_bytes=64)
-        for cols in (slice(0, 128), slice(128, 256), slice(256, 512)):
+        for cols in (slice(c, c + 128) for c in range(0, S, 128)):
             nc.vector.quantize_mx(out=x_codes[:, cols].bitcast(FP8X4), scales=x_scales[:, cols], in_=x_grouped[:, cols].rearrange("p s j -> p (s j)"))
 
         w_dealt = w_f32[:].rearrange("p (j m t) -> p m j t", j=PACK, t=PACK)

@@ -78,17 +78,17 @@ def tile_picked_ranknet_sigmoid_lo_kernel(tc, xT, w1, offs, win, lose, out_0, ou
             pick(PACK - 1, cols)
         for cols in rest_pieces:
             lay_in(cols)
-        x_codes = keep.tile([P, S], U32, name="x_codes", align_bytes=64)
-        x_scales = keep.tile([P, S], U8, name="x_scales", align_bytes=64)
+        x_codes = keep.tile([P, S], U32, name="x_codes", align_bytes=256)
+        x_scales = keep.tile([P, S], U8, name="x_scales", align_bytes=256)
         for cols in (slice(c, c + 128) for c in range(0, S, 128)):
             nc.vector.quantize_mx(out=x_codes[:, cols].bitcast(FP8X4), scales=x_scales[:, cols], in_=x_grouped[:, cols].rearrange("p s j -> p (s j)"))
 
         w_dealt = w_f32[:].rearrange("p (j m t) -> p m j t", j=PACK, t=PACK)
         w_grouped = [keep.tile([P, 2, M_TILE, PACK], BF16, name="w_grouped_%d" % pair, align_bytes=64) for pair in range(2)]
-        w_codes = [keep.tile([P, M_TILE], U32, name="w_codes_%d" % t, align_bytes=64) for t in range(2)]
-        w_scales = [keep.tile([P, M_TILE], U8, name="w_scales_%d" % t, align_bytes=64) for t in range(2)]
-        late_codes = keep.tile([P, 2 * M_TILE], U32, name="late_codes", align_bytes=64)
-        late_scales = keep.tile([P, 2 * M_TILE], U8, name="late_scales", align_bytes=64)
+        w_codes = [keep.tile([P, M_TILE], U32, name="w_codes_%d" % t, align_bytes=256) for t in range(2)]
+        w_scales = [keep.tile([P, M_TILE], U8, name="w_scales_%d" % t, align_bytes=256) for t in range(2)]
+        late_codes = keep.tile([P, 2 * M_TILE], U32, name="late_codes", align_bytes=256)
+        late_scales = keep.tile([P, 2 * M_TILE], U8, name="late_scales", align_bytes=256)
 
         def deal(pair, start, split, stop):
             dst = w_grouped[pair][:].rearrange("p t m j -> p m j t")

@@ -175,8 +175,13 @@ def tile_picked_ranknet_sigmoid_lo_kernel(tc, xT, w1, offs, win, lose, out_0, ou
         out_codes = keep.tile([P, V], U32, name="out_codes", align_bytes=256)
         out_scales = keep.tile([P, V], U8, name="out_scales", align_bytes=64)
         words = out_1[0].rearrange("p v r -> p (v r)").bitcast(I32)
+
+        def weave(tiles, cols):
+            nc.vector.tensor_copy(by_twos(grouped[:, cols, tiles], "p (c i) t -> p c t i"), by_twos(prob[:, tiles, cols], "p t (c i) -> p c t i"))
+
+        weave(slice(0, 2), slice(0, last_pieces[1].stop))
         for cols in last_pieces[:2]:
-            nc.vector.tensor_copy(by_twos(grouped[:, cols, :], "p (c i) t -> p c t i"), by_twos(prob[:, :, cols], "p t (c i) -> p c t i"))
+            weave(slice(2, 4), cols)
         for cols in last_pieces:
             nc.vector.quantize_mx(out=out_codes[:, cols].bitcast(FP8X4), scales=out_scales[:, cols], in_=grouped[:, cols].rearrange("p v t -> p (v t)"))
         nc.sync.dma_start(words, out_codes[:].bitcast(I32))

@@ -161,16 +161,16 @@ def tile_picked_ranknet_sigmoid_lo_kernel(tc, xT, w1, offs, win, lose, out_0, ou
             nc.sync.dma_start(out_flat[:, start:stop], prob_flat[:, start:stop])
 
         nc.scalar.activation(prob[:, 0:2, :], margins[:, 0:2, :], ACT.Sigmoid)
+        store(0, 2 * V)
         fetch_margins(margins, 2, whole)
         nc.scalar.activation(prob[:, 2, :], margins[:, 2, :], ACT.Sigmoid)
-        store(0, 3 * V)
         for cols in last_pieces:
             fetch_margins(margins, 3, cols)
         nc.scalar.activation(prob[:, 3, halves[0]], margins[:, 3, halves[0]], ACT.Sigmoid)
         nc.scalar.activation(prob[:, 3, last_pieces[1]], margins[:, 3, last_pieces[1]], ACT.Sigmoid)
-        nc.scalar.activation(by_twos(grouped[:, last_pieces[2], :], "p (c i) t -> p c t i"), by_twos(margins[:, :, last_pieces[2]], "p t (c i) -> p c t i"), ACT.Sigmoid)
         nc.scalar.activation(prob[:, 3, last_pieces[2]], margins[:, 3, last_pieces[2]], ACT.Sigmoid)
-        store(3 * V, 4 * V)
+        store(2 * V, 4 * V)
+        nc.scalar.activation(by_twos(grouped[:, last_pieces[2], :], "p (c i) t -> p c t i"), by_twos(margins[:, :, last_pieces[2]], "p t (c i) -> p c t i"), ACT.Sigmoid)
 
         out_codes = keep.tile([P, V], U32, name="out_codes", align_bytes=256)
         out_scales = keep.tile([P, V], U8, name="out_scales", align_bytes=64)

@@ -58,26 +58,12 @@ def tile_picked_ranknet_sigmoid_lo_kernel(tc, xT, w1, offs, win, lose, out_0, ou
             return tile[:, cols.start // LIST_ROWS : cols.stop // LIST_ROWS]
 
         x_grouped = keep.tile([P, S, PACK], BF16, name="x_grouped", align_bytes=64)
-        shared = 320
-        picked = keep.tile([P, PACK, S - shared], BF16, name="picked")
-
-        def pick(j, cols):
-            nc.scalar.activation(picked[:, j, cols.start - shared : cols.stop - shared], x_f32[j][:].indirect(entries(offs_sb, cols)), ACT.Copy)
-
-        def lay_in(cols):
-            src = picked[:, :, cols.start - shared : cols.stop - shared]
-            nc.scalar.copy(x_grouped[:, cols, :].rearrange("p (c i) j -> p c j i", i=2), src.rearrange("p j (c i) -> p c j i", i=2))
-
+        shared = 256
         for j in range(PACK):
-            for cols in [slice(0, shared)] if j < PACK - 1 else [slice(0, 192), slice(192, shared)]:
+            for cols in [slice(0, shared)] if j < PACK - 1 else [slice(0, 128), slice(128, shared)]:
                 nc.vector.tensor_copy(x_grouped[:, cols, j], x_f32[j][:].indirect(entries(offs_sb, cols)))
-        rest_pieces = [slice(shared, 384), slice(384, S)]
-        for j in range(PACK - 1):
-            pick(j, slice(shared, S))
-        for cols in rest_pieces:
-            pick(PACK - 1, cols)
-        for cols in rest_pieces:
-            lay_in(cols)
+            for cols in [slice(shared, S)] if j < PACK - 1 else [slice(shared, 384), slice(384, S)]:
+                nc.scalar.activation(x_grouped[:, cols, j], x_f32[j][:].indirect(entries(offs_sb, cols)), ACT.Copy)
         x_codes = keep.tile([P, S], U32, name="x_codes", align_bytes=256)
         x_scales = keep.tile([P, S], U8, name="x_scales", align_bytes=256)
         for cols in (slice(c, c + 128) for c in range(0, S, 128)):

from contextlib import ExitStack

import concourse.mybir as mybir

K, T, S, V, N = 512, 1024, 512, 256, 512
FLOPS = 2 * K * N * S

F32 = mybir.dt.float32
BF16 = mybir.dt.bfloat16
I32 = mybir.dt.int32
U32 = mybir.dt.uint32
U16 = mybir.dt.uint16
U8 = mybir.dt.uint8
FP8X4 = mybir.dt.float8_e4m3fn_x4
ACT = mybir.ActivationFunctionType
SUB = mybir.AluOpType.subtract

P = 128
PACK = 4
M_TILE = 128
HALF_S = S // 2
HALF_V = V // 2
LIST_ROWS = 16


def tile_picked_ranknet_sigmoid_lo_kernel(tc, xT, w1, offs, win, lose, out_0, out_1, out_2):
    nc = tc.nc
    with ExitStack() as ctx:
        lists = ctx.enter_context(tc.tile_pool(name="lists", bufs=1))
        keep = ctx.enter_context(tc.tile_pool(name="keep", bufs=1))
        psum = ctx.enter_context(tc.psum_pool(name="psum", bufs=1))

        offs_sb = lists.tile([P, S // LIST_ROWS], U16, name="offs_sb")
        win_sb = lists.tile([P, V // LIST_ROWS], U16, name="win_sb")
        lose_sb = lists.tile([P, V // LIST_ROWS], U16, name="lose_sb")

        x_rows = xT.rearrange("(p j) t -> p j t", j=PACK)
        x_f32 = [keep.tile([P, T], F32, name="x_f32_%d" % j, align_bytes=256) for j in range(PACK)]
        w_f32 = keep.tile([P, PACK * N], F32, name="w_f32", align_bytes=256)
        w_rows = w1.rearrange("(p j) n -> p (j n)", j=PACK)
        early = PACK * N - N // 2
        load_order = (0, 1, 2, 3)
        nc.sync.dma_start(x_f32[0][:], x_rows[:, 0, :])
        nc.sync.dma_start(offs_sb[:], offs)
        for j in load_order[1:]:
            nc.sync.dma_start(x_f32[j][:], x_rows[:, j, :])
        nc.sync.dma_start(w_f32[:, :early], w_rows[:, :early])
        nc.sync.dma_start(lose_sb[:], lose)
        nc.sync.dma_start(w_f32[:, early:], w_rows[:, early:])
        nc.sync.dma_start(win_sb[:], win)

        warm_in = keep.tile([P, 1], F32, name="warm_in")
        warm_out = keep.tile([P, 1], F32, name="warm_out")
        nc.vector.memset(warm_in[:], 0.0)
        nc.scalar.activation(warm_out[:], warm_in[:], ACT.Sigmoid)

        def entries(tile, cols):
            return tile[:, cols.start // LIST_ROWS : cols.stop // LIST_ROWS]

        x_grouped = keep.tile([P, S, PACK], BF16, name="x_grouped", align_bytes=64)
        shared = 256
        for j in range(PACK):
            for cols in [slice(0, shared)] if j < PACK - 1 else [slice(0, 128), slice(128, shared)]:
                nc.vector.tensor_copy(x_grouped[:, cols, j], x_f32[j][:].indirect(entries(offs_sb, cols)))
            for cols in [slice(shared, S)] if j < PACK - 1 else [slice(shared, 384), slice(384, S)]:
                nc.scalar.activation(x_grouped[:, cols, j], x_f32[j][:].indirect(entries(offs_sb, cols)), ACT.Copy)
        x_codes = keep.tile([P, S], U32, name="x_codes", align_bytes=256)
        x_scales = keep.tile([P, S], U8, name="x_scales", align_bytes=256)
        for cols in (slice(c, c + 128) for c in range(0, S, 128)):
            nc.vector.quantize_mx(out=x_codes[:, cols].bitcast(FP8X4), scales=x_scales[:, cols], in_=x_grouped[:, cols].rearrange("p s j -> p (s j)"))

        w_dealt = w_f32[:].rearrange("p (j m t) -> p m j t", j=PACK, t=PACK)
        w_grouped = [keep.tile([P, 2, M_TILE, PACK], BF16, name="w_grouped_%d" % pair, align_bytes=64) for pair in range(2)]
        w_codes = [keep.tile([P, M_TILE], U32, name="w_codes_%d" % t, align_bytes=256) for t in range(2)]
        w_scales = [keep.tile([P, M_TILE], U8, name="w_scales_%d" % t, align_bytes=256) for t in range(2)]
        late_codes = keep.tile([P, 2 * M_TILE], U32, name="late_codes", align_bytes=256)
        late_scales = keep.tile([P, 2 * M_TILE], U8, name="late_scales", align_bytes=256)

        def deal(pair, start, split, stop):
            dst = w_grouped[pair][:].rearrange("p t m j -> p m j t")
            src = w_dealt[:, :, :, 2 * pair : 2 * pair + 2]
            nc.vector.tensor_copy(dst[:, start:split], src[:, start:split])
            nc.scalar.copy(dst[:, split:stop], src[:, split:stop])

        deal(0, 0, 38, 64)
        deal(0, 64, 102, 128)
        for t in range(2):
            nc.vector.quantize_mx(out=w_codes[t][:].bitcast(FP8X4), scales=w_scales[t][:], in_=w_grouped[0][:, t].rearrange("p m j -> p (m j)"))
        deal(1, 0, 76, 128)
        nc.vector.quantize_mx(out=late_codes[:].bitcast(FP8X4), scales=late_scales[:], in_=w_grouped[1][:].rearrange("p t m j -> p (t m j)"))
        stationary = [(w_codes[t][:], w_scales[t][:]) for t in range(2)]
        stationary = stationary + [(late_codes[:, u * M_TILE : (u + 1) * M_TILE], late_scales[:, u * M_TILE : (u + 1) * M_TILE]) for u in range(2)]

        def product(acc, t, cols):
            nc.tensor.matmul_mx(
                out=acc,
                lhsT=stationary[t][0].bitcast(FP8X4),
                lhsT_scale=stationary[t][1],
                rhs=x_codes[:, cols].bitcast(FP8X4),
                rhs_scale=x_scales[:, cols],
                start=True,
                stop=True,
            )

        y = [keep.tile([P, S], F32, name="y_%d" % t) for t in range(PACK)]

        def scores(t, pieces):
            for h, (cols, copy, bank) in enumerate(pieces):
                acc = psum.tile([P, cols.stop - cols.start], F32, name="acc_%d_%d" % (t, h), tag="bank_%d" % bank)
                product(acc[:], t, cols)
                copy(y[t][:, cols], acc[:])

        front, back = slice(0, HALF_S), slice(HALF_S, S)

        losers = [keep.tile([P, V], F32, name="losers_%d" % t, tag="losers_%d" % t) for t in range(PACK)]
        prob = keep.tile([P, PACK, V], F32, name="prob", align_bytes=256)

        grouped = keep.tile([P, V, PACK], BF16, name="prob_grouped", align_bytes=64)
        halves = [slice(h * HALF_V, (h + 1) * HALF_V) for h in range(2)]
        last_pieces = [slice(0, 128), slice(128, 192), slice(192, 256)]

        def fetch_losers_scalar(t, cols):
            nc.scalar.activation(losers[t][:, cols], y[t][:].indirect(entries(lose_sb, cols)), ACT.Copy)

        def fetch_margins(margins, t, cols):
            nc.vector.tensor_tensor(margins[:, t, cols], y[t][:].indirect(entries(win_sb, cols)), losers[t][:, cols], SUB)

        def by_twos(view, pattern):
            return view.rearrange(pattern, i=2)

        whole = slice(0, V)
        margins = keep.tile([P, PACK, V], F32, name="margins", align_bytes=64)
        scores(0, [(slice(0, 256), nc.vector.tensor_copy, 0), (slice(256, 384), nc.scalar.copy, 1), (slice(384, 512), nc.scalar.copy, 2)])
        scores(1, [(front, nc.vector.tensor_copy, 3), (back, nc.vector.tensor_copy, 4)])
        fetch_losers_scalar(0, whole)
        scores(2, [(front, nc.vector.tensor_copy, 5), (back, nc.vector.tensor_copy, 6)])
        fetch_losers_scalar(1, whole)
        scores(3, [(front, nc.vector.tensor_copy, 7), (back, nc.scalar.copy, 4)])
        fetch_margins(margins, 0, whole)
        fetch_losers_scalar(2, whole)
        fetch_losers_scalar(3, whole)
        fetch_margins(margins, 1, whole)
        out_flat = out_0.rearrange("(p t) v -> p (t v)", t=PACK)
        prob_flat = prob[:].rearrange("p t v -> p (t v)")

        def store(start, stop):
            nc.sync.dma_start(out_flat[:, start:stop], prob_flat[:, start:stop])

        nc.scalar.activation(prob[:, 0:2, :], margins[:, 0:2, :], ACT.Sigmoid)
        store(0, 2 * V)
        fetch_margins(margins, 2, whole)
        nc.scalar.activation(prob[:, 2, :], margins[:, 2, :], ACT.Sigmoid)
        for cols in last_pieces:
            fetch_margins(margins, 3, cols)
        nc.scalar.activation(prob[:, 3, halves[0]], margins[:, 3, halves[0]], ACT.Sigmoid)
        nc.scalar.activation(prob[:, 3, last_pieces[1]], margins[:, 3, last_pieces[1]], ACT.Sigmoid)
        nc.scalar.activation(prob[:, 3, last_pieces[2]], margins[:, 3, last_pieces[2]], ACT.Sigmoid)
        store(2 * V, 4 * V)
        nc.scalar.activation(by_twos(grouped[:, last_pieces[2], :], "p (c i) t -> p c t i"), by_twos(margins[:, :, last_pieces[2]], "p t (c i) -> p c t i"), ACT.Sigmoid)

        out_codes = keep.tile([P, V], U32, name="out_codes", align_bytes=256)
        out_scales = keep.tile([P, V], U8, name="out_scales", align_bytes=64)
        words = out_1[0].rearrange("p v r -> p (v r)").bitcast(I32)

        def weave(tiles, cols):
            nc.vector.tensor_copy(by_twos(grouped[:, cols, tiles], "p (c i) t -> p c t i"), by_twos(prob[:, tiles, cols], "p t (c i) -> p c t i"))

        weave(slice(0, 2), slice(0, last_pieces[1].stop))
        for cols in last_pieces[:2]:
            weave(slice(2, 4), cols)
        for cols in last_pieces:
            nc.vector.quantize_mx(out=out_codes[:, cols].bitcast(FP8X4), scales=out_scales[:, cols], in_=grouped[:, cols].rearrange("p v t -> p (v t)"))
        nc.sync.dma_start(words, out_codes[:].bitcast(I32))
        for q, queue in enumerate((nc.scalar, nc.scalar, nc.sync, nc.sync)):
            queue.dma_start(out_2[0, 4 * q : 4 * q + 4, :].bitcast(I32), out_scales[32 * q : 32 * q + 4, :].bitcast(I32))
